import numpy as np
import ml_dtypes


def mxq(x, axis, fmt="e4m3"):
    dtype, down = {"e4m3": (ml_dtypes.float8_e4m3fn, 7), "e5m2": (ml_dtypes.float8_e5m2, 14)}[fmt]
    v = np.moveaxis(np.asarray(x, np.float32).astype(ml_dtypes.bfloat16).astype(np.float64), axis, -1)
    blocks = v.reshape(v.shape[:-1] + (-1, 32))
    amax = np.abs(blocks).max(-1, keepdims=True)
    byte = np.maximum(np.where(amax > 0, np.frexp(amax)[1] - 1 + 127, 0) - down, 1)
    scale = np.exp2(byte - 127.0)
    codes = (blocks / scale).astype(np.float32).astype(dtype).astype(np.float64)
    return np.moveaxis((codes * scale).reshape(v.shape), -1, axis)


WIDE = False


def mx_kscale(k):
    if not WIDE:
        return np.ones(k)
    levels = np.array([10, -10, 5, -5, 0])
    if k % 512:
        return np.exp2(np.random.permutation(np.resize(levels, k // 32))).repeat(32)
    a = np.empty((k // 512, 16))
    for p in range(k // 512):
        a[p, :8] = np.random.permutation(np.resize(levels, 8))
        for g in range(8):
            far = levels[np.abs(levels - a[p, g]) >= 10]
            a[p, g + 8] = far[np.random.randint(len(far))]
    return np.exp2(a.ravel()).repeat(32)


BF16 = ml_dtypes.bfloat16


def bf(x):
    return np.asarray(x, np.float32).astype(BF16)


def f64(x):
    return np.asarray(x).astype(np.float64)


E2M1 = np.array([0.0, 0.5, 1.0, 1.5, 2.0, 3.0, 4.0, 6.0, -0.0, -0.5, -1.0, -1.5, -2.0, -3.0, -4.0, -6.0])


def pack_weight(w, fmt):
    k, n = w.shape
    w = f64(bf(w)).reshape(k // 32, 32, n)
    amax = np.abs(w).max(1)
    if fmt == "e4m3":
        byte = np.frexp(amax)[1] - 1 + 127 - 7
    else:
        mant, ex = np.frexp(amax / 6.0)
        byte = np.where(mant > 0.5, ex, ex - 1) + 127
    byte = np.clip(np.where(amax > 0, byte, 1), 1, 254)
    scaled = (w * np.exp2(127.0 - byte)[:, None, :]).reshape(k, n).astype(np.float32)
    by_word = np.ascontiguousarray(scaled.reshape(k // 512, 128, 4, n).transpose(0, 1, 3, 2))
    if fmt == "e4m3":
        words = by_word.astype(ml_dtypes.float8_e4m3fn).view(np.uint8)
    else:
        c = by_word.astype(ml_dtypes.float4_e2m1fn).view(np.uint8) & 0xF
        words = c[..., 0::2] | (c[..., 1::2] << 4)
    return np.ascontiguousarray(words), np.ascontiguousarray(byte.astype(np.uint8).reshape(k // 512, 16, n))


def unpack_weight(words, scales, fmt):
    g, p, n, _ = words.shape
    if fmt == "e4m3":
        vals = np.ascontiguousarray(words).view(ml_dtypes.float8_e4m3fn).astype(np.float64)
    else:
        nib = np.empty((g, p, n, 4), np.uint8)
        nib[..., 0::2] = words & 0xF
        nib[..., 1::2] = words >> 4
        vals = E2M1[nib]
    vals = vals * np.repeat(np.exp2(scales.astype(np.float64) - 127.0), 8, axis=1)[..., None]
    return vals.transpose(0, 1, 3, 2).reshape(g * 512, n)
def pack4(w):
    words, scales = pack_weight(w, "e2m1")
    return words.reshape(words.shape[0], 128, -1), scales


def unpack4(words, scales):
    return unpack_weight(words.reshape(words.shape[0], 128, -1, 2), scales, "e2m1")


E4M3FN = np.array([(-1.0 if i & 128 else 1.0) * ((1.0 + (i & 7) / 8.0) * 2.0 ** (((i >> 3) & 15) - 7) if i & 120 else (i & 7) * 2.0 ** -9) for i in range(256)])


def e4m3fn_bytes(y):
    return np.clip(np.asarray(y, np.float64), -448.0, 448.0).astype(np.float32).astype(ml_dtypes.float8_e4m3fn).view(np.uint8)


def e4m3fn_values(b):
    return E4M3FN[b]


T, K, F, B = 512, 1024, 4096, 128


def setup_inputs():
    s, t = mx_kscale(K), mx_kscale(F)
    x = np.random.standard_normal((T, K)) * s
    x_scale = (np.abs(x).reshape(T, K // B, B).max(axis=2) / 448.0).astype(np.float32)
    x_bytes = e4m3fn_bytes(x / np.repeat(f64(x_scale), B, axis=1))
    w_enc = np.random.standard_normal((F, K)) / np.sqrt(K) / s * t[:, None]
    w_dec = np.random.standard_normal((F, K)) / np.sqrt(F) / t[:, None]
    dec_words, dec_scales = pack4(w_dec)
    return {"x_bytes": x_bytes,
            "x_scale": x_scale,
            "w_enc": bf(w_enc),
            "b_enc": bf(0.5 * np.random.standard_normal(F) * t),
            "dec_words": dec_words,
            "dec_scales": dec_scales,
            "b_dec": bf(0.3 * np.random.standard_normal(K))}


def reference(x_bytes, x_scale, w_enc, b_enc, dec_words, dec_scales, b_dec):
    x = e4m3fn_values(x_bytes) * np.repeat(f64(x_scale), B, axis=1)
    pre = mxq(x, 1, "e4m3") @ mxq(f64(w_enc), 1, "e4m3").T
    z = np.maximum(pre + f64(b_enc), 0.0)
    rec = mxq(z, 1, "e4m3") @ unpack4(dec_words, dec_scales)
    return rec + f64(b_dec)

@@ -1,0 +1,269 @@
+from contextlib import ExitStack
+
+import concourse.mybir as mybir
+from concourse.masks import make_identity
+
+T, K, F, B = 512, 1024, 4096, 128
+FLOPS = 2 * 2 * T * K * F
+
+F32 = mybir.dt.float32
+BF16 = mybir.dt.bfloat16
+I32 = mybir.dt.int32
+U32 = mybir.dt.uint32
+U8 = mybir.dt.uint8
+FP8 = mybir.dt.float8_e4m3fn
+FP8X4 = mybir.dt.float8_e4m3fn_x4
+FP4X4 = mybir.dt.float4_e2m1fn_x4
+ALU = mybir.AluOpType
+ACT = mybir.ActivationFunctionType
+
+P = 128
+GROUPS = F // 512
+PAIRS = F // 256
+EARLY = 2
+XV = 6
+DIRECT = 2
+
+
+def tile_sae_encode_decode_fp8_d4_kernel(tc, x_bytes, x_scale, w_enc, b_enc, dec_words, dec_scales, b_dec, out):
+    nc = tc.nc
+    with ExitStack() as ctx:
+        keep = ctx.enter_context(tc.tile_pool(name="keep", bufs=1))
+        wraw = ctx.enter_context(tc.tile_pool(name="wraw", bufs=PAIRS))
+        work = ctx.enter_context(tc.tile_pool(name="work", bufs=3))
+        outp = ctx.enter_context(tc.tile_pool(name="outp", bufs=4))
+        psum = ctx.enter_context(tc.psum_pool(name="psum", bufs=2))
+
+        ident = keep.tile([P, P], F32, name="ident")
+        dsc = keep.tile([P, GROUPS, K], U8, name="dsc", align_bytes=64)
+        dw = keep.tile([P, GROUPS, 2 * K], U8, name="dw", align_bytes=64)
+        zc = keep.tile([P, GROUPS, T], U32, name="zc", align_bytes=64)
+        zs = keep.tile([P, GROUPS, T], U8, name="zs", align_bytes=64)
+        xc = keep.tile([P, 2, T], U32, name="xc", align_bytes=64)
+        xs = keep.tile([P, 2, T], U8, name="xs", align_bytes=64)
+        xsc = keep.tile([P, 4, 8], F32, name="xsc")
+        b_bf = keep.tile([P, GROUPS, 4], BF16, name="b_bf")
+        b_f = keep.tile([P, GROUPS, 4], F32, name="b_f")
+        bd = keep.tile([P, K], BF16, name="bd")
+        xin = [keep.tile([P, 2, K], U8, name="xin%d" % i) for i in range(2)]
+
+        ctx.enter_context(tc.manual_schedule())
+
+        make_identity(nc, ident[:])
+        nc.vector.memset(dsc[:].rearrange("p g n -> p (g n)").bitcast(I32), 0)
+
+        nc.scalar.dma_start(out=xsc[:], in_=x_scale.rearrange("(n p) b -> p n b", p=P))
+        nc.scalar.dma_start(out=b_bf[:], in_=b_enc.rearrange("(g p t) -> p g t", p=P, t=4))
+
+        xr = x_bytes.rearrange("(i n p) k -> i p n k", p=P, n=2)
+        wr = w_enc.rearrange("(g m t) k -> g m t k", m=P, t=4)
+        raws = []
+
+        def load_w(j):
+            raw = wraw.tile([P, 2, K], BF16, name="raw")
+            t0 = 2 * (j % 2)
+            nc.sync.dma_start(out=raw[:], in_=wr[j // 2][:, t0 : t0 + 2, :])
+            raws.append(raw)
+
+        def load_dec(g):
+            nc.sync.dma_start(out=dw[:, g, :].bitcast(I32), in_=dec_words[g].bitcast(I32))
+
+        for i in range(2):
+            nc.sync.dma_start(out=xin[i][:], in_=xr[i])
+            if i == 0:
+                load_w(0)
+        for j in range(1, 6):
+            load_w(j)
+        for q in range(4):
+            nc.sync.dma_start(
+                out=dsc[32 * q : 32 * q + 4, :, :].bitcast(I32),
+                in_=dec_scales[:, 4 * q : 4 * q + 4, :].rearrange("g q n -> q g n").bitcast(I32),
+            )
+        load_dec(0)
+        for j in range(6, PAIRS):
+            load_w(j)
+            if j - 5 < GROUPS:
+                load_dec(j - 5)
+        nc.sync.dma_start(out=bd[:], in_=b_dec.partition_broadcast(P))
+
+        nc.scalar.copy(out=b_f[:], in_=b_bf[:])
+
+        xw, xg = {}, {}
+
+        def x_widen(n):
+            xw[n] = work.tile([P, K], BF16, name="xw", bufs=4)
+            for b in range(K // B):
+                src = xin[n // 2][:, n % 2, B * b : B * (b + 1)].bitcast(FP8)
+                dst = xw[n][:, B * b : B * (b + 1)]
+                s = xsc[:, n, b : b + 1]
+                if b < XV:
+                    nc.vector.tensor_scalar(out=dst, in0=src, scalar1=s, scalar2=None, op0=ALU.mult)
+                else:
+                    nc.scalar.activation(out=dst, in_=src, func=ACT.Copy, scale=s)
+
+        def words_out(dst, bank):
+            nc.scalar.copy(out=dst, in_=bank)
+
+        def x_turn(n):
+            tp = psum.tile([P, 2, 2, P], F32, name="tp", bufs=4)
+            words = xw[n][:].bitcast(F32)
+            for c in range(2):
+                for u in range(2):
+                    nc.tensor.transpose(tp[:, c, u, :], words[:, 256 * c + u : 256 * (c + 1) : 2], ident[:])
+            xg[n] = work.tile([P, 2, P, 4], BF16, name="xg", bufs=4, align_bytes=64)
+            dst = xg[n][:].rearrange("p c r t -> p (c r t)").bitcast(F32).rearrange("p (c r u) -> p c r u", c=2, u=2)
+            words_out(dst, tp[:].rearrange("p c u r -> p c r u"))
+
+        def x_quant(n):
+            for c in range(2):
+                nc.vector.quantize_mx(
+                    out=xc[:, c, P * n : P * (n + 1)].bitcast(FP8X4),
+                    scales=xs[:, c, P * n : P * (n + 1)],
+                    in_=xg[n][:, c, :, :].rearrange("p r t -> p (r t)"),
+                )
+
+        perm, wg, wc, ws = {}, {}, {}, {}
+
+        def w_perm(j):
+            perm[j] = work.tile([P, 2, 2, 2, P], F32, name="perm")
+            nc.vector.tensor_copy(
+                out=perm[j][:].rearrange("p f c u m -> p (f c) u m"),
+                in_=raws[j][:].rearrange("p f k -> p (f k)").bitcast(F32).rearrange("p (x m u) -> p x u m", m=P, u=2),
+            )
+
+        def w_turn(j):
+            wg[j] = work.tile([P, 2, 2, P, 4], BF16, name="wg", align_bytes=64)
+            for f in range(2):
+                tp = psum.tile([P, 2, 2, P], F32, name="tp", bufs=4)
+                for c in range(2):
+                    for u in range(2):
+                        if j < DIRECT:
+                            words = raws[j][:, f, :].bitcast(F32)
+                            nc.tensor.transpose(tp[:, c, u, :], words[:, 256 * c + u : 256 * (c + 1) : 2], ident[:])
+                        else:
+                            nc.tensor.transpose(tp[:, c, u, :], perm[j][:, f, c, u, :], ident[:])
+                dst = wg[j][:, f].rearrange("p c r t -> p (c r t)").bitcast(F32).rearrange("p (c r u) -> p c r u", c=2, u=2)
+                words_out(dst, tp[:].rearrange("p c u r -> p c r u"))
+
+        def w_quant(j):
+            wc[j] = work.tile([P, 4, P], U32, name="wc", align_bytes=64)
+            ws[j] = work.tile([P, 4, P], U8, name="ws", align_bytes=64)
+            nc.vector.quantize_mx(
+                out=wc[j][:].rearrange("p x r -> p (x r)").bitcast(FP8X4),
+                scales=ws[j][:].rearrange("p x r -> p (x r)"),
+                in_=wg[j][:].rearrange("p f c r t -> p (f c r t)"),
+            )
+
+        zt, zi = {}, {}
+
+        zp = {}
+
+        def encode(j, lo=0, hi=T):
+            g = j // 2
+            if j % 2 == 0 and lo == 0:
+                zt[g] = work.tile([P, 4, T], BF16, name="zt")
+            for f in range(2):
+                t = 2 * (j % 2) + f
+                if lo == 0:
+                    zp[f] = psum.tile([P, T], F32, name="zp", bufs=2)
+                for c in range(2):
+                    nc.tensor.matmul_mx(
+                        out=zp[f][:, lo:hi],
+                        lhsT=wc[j][:, 2 * f + c, :].bitcast(FP8X4),
+                        lhsT_scale=ws[j][:, 2 * f + c, :],
+                        rhs=xc[:, c, lo:hi].bitcast(FP8X4),
+                        rhs_scale=xs[:, c, lo:hi],
+                        start=(c == 0),
+                        stop=(c == 1),
+                    )
+                if hi == T:
+                    nc.scalar.activation(out=zt[g][:, t, :], in_=zp[f][:], func=ACT.Relu, bias=b_f[:, g, t : t + 1], scale=1.0)
+
+        def z_lace(g, h):
+            zi[g, h] = work.tile([P, 256, 4], BF16, name="zi", align_bytes=64)
+            nc.vector.tensor_copy(out=zi[g, h][:], in_=zt[g][:, :, 256 * h : 256 * (h + 1)].rearrange("p t n -> p n t"))
+
+        def z_quant(g, h):
+            nc.vector.quantize_mx(
+                out=zc[:, g, 256 * h : 256 * (h + 1)].bitcast(FP8X4),
+                scales=zs[:, g, 256 * h : 256 * (h + 1)],
+                in_=zi[g, h][:].rearrange("p n t -> p (n t)"),
+            )
+
+        acc = {}
+
+        def decode(g, b):
+            n, h = b // 2, b % 2
+            if g == 0:
+                name, bufs = ("rp", EARLY) if b < EARLY else (("tp", 4) if b < EARLY + 4 else ("zp", 2))
+                acc[b] = psum.tile([P, 512], F32, name="acc", tag=name, bufs=bufs)
+            nc.tensor.matmul_mx(
+                out=acc[b][:],
+                lhsT=zc[:, g, P * n : P * (n + 1)].bitcast(FP8X4),
+                lhsT_scale=zs[:, g, P * n : P * (n + 1)],
+                rhs=dw[:, g, 1024 * h : 1024 * (h + 1)].bitcast(FP4X4),
+                rhs_scale=dsc[:, g, 512 * h : 512 * (h + 1)],
+                start=(g == 0),
+                stop=(g == GROUPS - 1),
+            )
+
+        def store(b, cuts):
+            n, h = b // 2, b % 2
+            w = 512 // cuts
+            for i in range(cuts):
+                o = outp.tile([P, 512], F32, name="o")
+                nc.vector.tensor_tensor(
+                    out=o[:, 0:w], in0=acc[b][:, w * i : w * (i + 1)], in1=bd[:, 512 * h + w * i : 512 * h + w * (i + 1)], op=ALU.add
+                )
+                nc.sync.dma_start(out=out[P * n : P * (n + 1), 512 * h + w * i : 512 * h + w * (i + 1)], in_=o[:, 0:w])
+
+        x_widen(0)
+        x_widen(1)
+        x_turn(0)
+        x_widen(2)
+        x_turn(1)
+        x_quant(0)
+        x_widen(3)
+        w_turn(0)
+        x_quant(1)
+        x_turn(2)
+        w_quant(0)
+        w_perm(2)
+        x_turn(3)
+        x_quant(2)
+        w_turn(1)
+        x_quant(3)
+        encode(0, 0, 256)
+        encode(0, 256, 512)
+        w_quant(1)
+        w_perm(3)
+
+        for i in range(2, PAIRS + 3):
+            if i < PAIRS:
+                w_turn(i)
+            if i < PAIRS:
+                encode(i - 1)
+            if i + 2 < PAIRS and i + 2 >= 4:
+                w_perm(i + 2)
+            if i >= 3:
+                z_lace((i - 3) // 2, (i - 3) % 2)
+            if i < PAIRS:
+                w_quant(i)
+            if i >= 3:
+                z_quant((i - 3) // 2, (i - 3) % 2)
+            if i >= 4 and (i - 4) // 2 < GROUPS - 1:
+                for b in range(EARLY):
+                    if b % 2 == i % 2:
+                        decode((i - 4) // 2, b)
+            if i == PAIRS:
+                encode(i - 1)
+        for b in range(EARLY, EARLY + 4):
+            for g in range(GROUPS - 1):
+                decode(g, b)
+        for b in range(EARLY + 4):
+            decode(GROUPS - 1, b)
+            store(b, 1)
+        for b in range(EARLY + 4, 8):
+            for g in range(GROUPS):
+                decode(g, b)
+            store(b, 2 if b == 7 else 1)

@@ -20,7 +20,8 @@ ACT = mybir.ActivationFunctionType
 P = 128
 GROUPS = F // 512
 PAIRS = F // 256
-EARLY = 2
+EARLY = 4
+TB = min(4, 6 - EARLY)
 XV = 6
 DIRECT = 2
 
@@ -52,10 +53,9 @@ def tile_sae_encode_decode_fp8_d4_kernel(tc, x_bytes, x_scale, w_enc, b_enc, dec
         make_identity(nc, ident[:])
         nc.vector.memset(dsc[:].rearrange("p g n -> p (g n)").bitcast(I32), 0)
 
-        nc.scalar.dma_start(out=xsc[:], in_=x_scale.rearrange("(n p) b -> p n b", p=P))
-        nc.scalar.dma_start(out=b_bf[:], in_=b_enc.rearrange("(g p t) -> p g t", p=P, t=4))
+        nc.sync.dma_start(out=xsc[:], in_=x_scale.rearrange("(p n) b -> p n b", p=P))
 
-        xr = x_bytes.rearrange("(i n p) k -> i p n k", p=P, n=2)
+        xr = x_bytes.rearrange("(p i n) k -> i p n k", p=P, n=2)
         wr = w_enc.rearrange("(g m t) k -> g m t k", m=P, t=4)
         raws = []
 
@@ -86,7 +86,6 @@ def tile_sae_encode_decode_fp8_d4_kernel(tc, x_bytes, x_scale, w_enc, b_enc, dec
                 load_dec(j - 5)
         nc.sync.dma_start(out=bd[:], in_=b_dec.partition_broadcast(P))
 
-        nc.scalar.copy(out=b_f[:], in_=b_bf[:])
 
         xw, xg = {}, {}
 
@@ -105,7 +104,7 @@ def tile_sae_encode_decode_fp8_d4_kernel(tc, x_bytes, x_scale, w_enc, b_enc, dec
             nc.scalar.copy(out=dst, in_=bank)
 
         def x_turn(n):
-            tp = psum.tile([P, 2, 2, P], F32, name="tp", bufs=4)
+            tp = psum.tile([P, 2, 2, P], F32, name="xp", tag="rp", bufs=EARLY)
             words = xw[n][:].bitcast(F32)
             for c in range(2):
                 for u in range(2):
@@ -134,7 +133,7 @@ def tile_sae_encode_decode_fp8_d4_kernel(tc, x_bytes, x_scale, w_enc, b_enc, dec
         def w_turn(j):
             wg[j] = work.tile([P, 2, 2, P, 4], BF16, name="wg", align_bytes=64)
             for f in range(2):
-                tp = psum.tile([P, 2, 2, P], F32, name="tp", bufs=4)
+                tp = psum.tile([P, 2, 2, P], F32, name="tp", bufs=TB)
                 for c in range(2):
                     for u in range(2):
                         if j < DIRECT:
@@ -165,7 +164,7 @@ def tile_sae_encode_decode_fp8_d4_kernel(tc, x_bytes, x_scale, w_enc, b_enc, dec
             for f in range(2):
                 t = 2 * (j % 2) + f
                 if lo == 0:
-                    zp[f] = psum.tile([P, T], F32, name="zp", bufs=2)
+                    zp[f] = psum.tile([P, T], F32, name="zp", bufs=8 - EARLY - TB)
                 for c in range(2):
                     nc.tensor.matmul_mx(
                         out=zp[f][:, lo:hi],
@@ -191,11 +190,12 @@ def tile_sae_encode_decode_fp8_d4_kernel(tc, x_bytes, x_scale, w_enc, b_enc, dec
             )
 
         acc = {}
+        orows = out.rearrange("(p n) k -> n p k", p=P)
 
         def decode(g, b):
             n, h = b // 2, b % 2
             if g == 0:
-                name, bufs = ("rp", EARLY) if b < EARLY else (("tp", 4) if b < EARLY + 4 else ("zp", 2))
+                name, bufs = ("rp", EARLY) if b < EARLY else (("tp", TB) if b < EARLY + TB else ("zp", 8 - EARLY - TB))
                 acc[b] = psum.tile([P, 512], F32, name="acc", tag=name, bufs=bufs)
             nc.tensor.matmul_mx(
                 out=acc[b][:],
@@ -215,9 +215,10 @@ def tile_sae_encode_decode_fp8_d4_kernel(tc, x_bytes, x_scale, w_enc, b_enc, dec
                 nc.vector.tensor_tensor(
                     out=o[:, 0:w], in0=acc[b][:, w * i : w * (i + 1)], in1=bd[:, 512 * h + w * i : 512 * h + w * (i + 1)], op=ALU.add
                 )
-                nc.sync.dma_start(out=out[P * n : P * (n + 1), 512 * h + w * i : 512 * h + w * (i + 1)], in_=o[:, 0:w])
+                nc.sync.dma_start(out=orows[n][:, 512 * h + w * i : 512 * h + w * (i + 1)], in_=o[:, 0:w])
 
         x_widen(0)
+        nc.scalar.dma_start(out=b_bf[:], in_=b_enc.rearrange("(g p t) -> p g t", p=P, t=4))
         x_widen(1)
         x_turn(0)
         x_widen(2)
@@ -228,10 +229,11 @@ def tile_sae_encode_decode_fp8_d4_kernel(tc, x_bytes, x_scale, w_enc, b_enc, dec
         x_quant(1)
         x_turn(2)
         w_quant(0)
-        w_perm(2)
         x_turn(3)
+        w_perm(2)
         x_quant(2)
         w_turn(1)
+        nc.scalar.copy(out=b_f[:], in_=b_bf[:])
         x_quant(3)
         encode(0, 0, 256)
         encode(0, 256, 512)
@@ -241,13 +243,15 @@ def tile_sae_encode_decode_fp8_d4_kernel(tc, x_bytes, x_scale, w_enc, b_enc, dec
         for i in range(2, PAIRS + 3):
             if i < PAIRS:
                 w_turn(i)
-            if i < PAIRS:
+            if i <= PAIRS:
                 encode(i - 1)
             if i + 2 < PAIRS and i + 2 >= 4:
                 w_perm(i + 2)
+            if 14 <= i < PAIRS:
+                w_quant(i)
             if i >= 3:
                 z_lace((i - 3) // 2, (i - 3) % 2)
-            if i < PAIRS:
+            if i < 14:
                 w_quant(i)
             if i >= 3:
                 z_quant((i - 3) // 2, (i - 3) % 2)
@@ -255,15 +259,13 @@ def tile_sae_encode_decode_fp8_d4_kernel(tc, x_bytes, x_scale, w_enc, b_enc, dec
                 for b in range(EARLY):
                     if b % 2 == i % 2:
                         decode((i - 4) // 2, b)
-            if i == PAIRS:
-                encode(i - 1)
-        for b in range(EARLY, EARLY + 4):
+        for b in range(EARLY, EARLY + TB):
             for g in range(GROUPS - 1):
                 decode(g, b)
-        for b in range(EARLY + 4):
+        for b in range(EARLY + TB):
             decode(GROUPS - 1, b)
             store(b, 1)
-        for b in range(EARLY + 4, 8):
+        for b in range(EARLY + TB, 8):
             for g in range(GROUPS):
                 decode(g, b)
             store(b, 2 if b == 7 else 1)

@@ -20,8 +20,11 @@ ACT = mybir.ActivationFunctionType
 P = 128
 GROUPS = F // 512
 PAIRS = F // 256
-EARLY = 4
-TB = min(4, 6 - EARLY)
+CHUNK = 2
+ZB = 2
+PA = 1
+EARLY = 8 - CHUNK - ZB
+TB = CHUNK
 XV = 6
 DIRECT = 2
 
@@ -51,6 +54,14 @@ def tile_sae_encode_decode_fp8_d4_kernel(tc, x_bytes, x_scale, w_enc, b_enc, dec
         ctx.enter_context(tc.manual_schedule())
 
         make_identity(nc, ident[:])
+        warm = keep.tile([P, 512], BF16, name="warm")
+        nc.vector.memset(warm[:], 0.0)
+
+        def warm_up(n):
+            for i in range(n):
+                wp = psum.tile([P, T], F32, name="wp", tag="zp", bufs=ZB)
+                nc.tensor.matmul(wp[:], lhsT=warm[:, 0:P], rhs=warm[:], start=True, stop=True)
+
         nc.vector.memset(dsc[:].rearrange("p g n -> p (g n)").bitcast(I32), 0)
 
         nc.sync.dma_start(out=xsc[:], in_=x_scale.rearrange("(p n) b -> p n b", p=P))
@@ -100,10 +111,13 @@ def tile_sae_encode_decode_fp8_d4_kernel(tc, x_bytes, x_scale, w_enc, b_enc, dec
                 else:
                     nc.scalar.activation(out=dst, in_=src, func=ACT.Copy, scale=s)
 
-        def words_out(dst, bank):
-            nc.scalar.copy(out=dst, in_=bank)
+        def words_out(dst, bank, eng="s"):
+            if eng == "s":
+                nc.scalar.copy(out=dst, in_=bank)
+            else:
+                nc.vector.tensor_copy(out=dst, in_=bank)
 
-        def x_turn(n):
+        def x_turn(n, eng="s"):
             tp = psum.tile([P, 2, 2, P], F32, name="xp", tag="rp", bufs=EARLY)
             words = xw[n][:].bitcast(F32)
             for c in range(2):
@@ -111,7 +125,7 @@ def tile_sae_encode_decode_fp8_d4_kernel(tc, x_bytes, x_scale, w_enc, b_enc, dec
                     nc.tensor.transpose(tp[:, c, u, :], words[:, 256 * c + u : 256 * (c + 1) : 2], ident[:])
             xg[n] = work.tile([P, 2, P, 4], BF16, name="xg", bufs=4, align_bytes=64)
             dst = xg[n][:].rearrange("p c r t -> p (c r t)").bitcast(F32).rearrange("p (c r u) -> p c r u", c=2, u=2)
-            words_out(dst, tp[:].rearrange("p c u r -> p c r u"))
+            words_out(dst, tp[:].rearrange("p c u r -> p c r u"), eng)
 
         def x_quant(n):
             for c in range(2):
@@ -123,63 +137,59 @@ def tile_sae_encode_decode_fp8_d4_kernel(tc, x_bytes, x_scale, w_enc, b_enc, dec
 
         perm, wg, wc, ws = {}, {}, {}, {}
 
-        def w_perm(j):
-            perm[j] = work.tile([P, 2, 2, 2, P], F32, name="perm")
-            nc.vector.tensor_copy(
-                out=perm[j][:].rearrange("p f c u m -> p (f c) u m"),
-                in_=raws[j][:].rearrange("p f k -> p (f k)").bitcast(F32).rearrange("p (x m u) -> p x u m", m=P, u=2),
-            )
+        def raw_words(f):
+            return raws[f // 2][:, f % 2, :].bitcast(F32)
 
-        def w_turn(j):
-            wg[j] = work.tile([P, 2, 2, P, 4], BF16, name="wg", align_bytes=64)
-            for f in range(2):
-                tp = psum.tile([P, 2, 2, P], F32, name="tp", bufs=TB)
-                for c in range(2):
-                    for u in range(2):
-                        if j < DIRECT:
-                            words = raws[j][:, f, :].bitcast(F32)
-                            nc.tensor.transpose(tp[:, c, u, :], words[:, 256 * c + u : 256 * (c + 1) : 2], ident[:])
-                        else:
-                            nc.tensor.transpose(tp[:, c, u, :], perm[j][:, f, c, u, :], ident[:])
-                dst = wg[j][:, f].rearrange("p c r t -> p (c r t)").bitcast(F32).rearrange("p (c r u) -> p c r u", c=2, u=2)
-                words_out(dst, tp[:].rearrange("p c u r -> p c r u"))
+        def w_perm(f):
+            perm[f] = work.tile([P, 2, 2, P], F32, name="perm", bufs=6)
+            nc.vector.tensor_copy(out=perm[f][:], in_=raw_words(f).rearrange("p (c m u) -> p c u m", m=P, u=2))
 
-        def w_quant(j):
-            wc[j] = work.tile([P, 4, P], U32, name="wc", align_bytes=64)
-            ws[j] = work.tile([P, 4, P], U8, name="ws", align_bytes=64)
+        def w_turn(f, direct=False, eng="s", tag="tp", bufs=TB):
+            wg[f] = work.tile([P, 2, P, 4], BF16, name="wg", align_bytes=64, bufs=8)
+            tp = psum.tile([P, 2, 2, P], F32, name="tp", tag=tag, bufs=bufs)
+            for c in range(2):
+                for u in range(2):
+                    src = raw_words(f)[:, 256 * c + u : 256 * (c + 1) : 2] if direct else perm[f][:, c, u, :]
+                    nc.tensor.transpose(tp[:, c, u, :], src, ident[:])
+            dst = wg[f][:].rearrange("p c r t -> p (c r t)").bitcast(F32).rearrange("p (c r u) -> p c r u", c=2, u=2)
+            words_out(dst, tp[:].rearrange("p c u r -> p c r u"), eng)
+
+        def w_quant(f):
+            wc[f] = work.tile([P, 2, P], U32, name="wc", align_bytes=64, bufs=8)
+            ws[f] = work.tile([P, 2, P], U8, name="ws", align_bytes=64, bufs=8)
             nc.vector.quantize_mx(
-                out=wc[j][:].rearrange("p x r -> p (x r)").bitcast(FP8X4),
-                scales=ws[j][:].rearrange("p x r -> p (x r)"),
-                in_=wg[j][:].rearrange("p f c r t -> p (f c r t)"),
+                out=wc[f][:].rearrange("p x r -> p (x r)").bitcast(FP8X4),
+                scales=ws[f][:].rearrange("p x r -> p (x r)"),
+                in_=wg[f][:].rearrange("p c r t -> p (c r t)"),
             )
 
         zt, zi = {}, {}
-
         zp = {}
 
-        def encode(j, lo=0, hi=T):
-            g = j // 2
-            if j % 2 == 0 and lo == 0:
+        def encode(f, lo=0, hi=T, eng="s"):
+            g, t = f // 4, f % 4
+            if t == 0 and lo == 0:
                 zt[g] = work.tile([P, 4, T], BF16, name="zt")
-            for f in range(2):
-                t = 2 * (j % 2) + f
-                if lo == 0:
-                    zp[f] = psum.tile([P, T], F32, name="zp", bufs=8 - EARLY - TB)
-                for c in range(2):
-                    nc.tensor.matmul_mx(
-                        out=zp[f][:, lo:hi],
-                        lhsT=wc[j][:, 2 * f + c, :].bitcast(FP8X4),
-                        lhsT_scale=ws[j][:, 2 * f + c, :],
-                        rhs=xc[:, c, lo:hi].bitcast(FP8X4),
-                        rhs_scale=xs[:, c, lo:hi],
-                        start=(c == 0),
-                        stop=(c == 1),
-                    )
-                if hi == T:
+            if lo == 0:
+                zp[f] = psum.tile([P, T], F32, name="zp", bufs=ZB)
+            for c in range(2):
+                nc.tensor.matmul_mx(
+                    out=zp[f][:, lo:hi],
+                    lhsT=wc[f][:, c, :].bitcast(FP8X4),
+                    lhsT_scale=ws[f][:, c, :],
+                    rhs=xc[:, c, lo:hi].bitcast(FP8X4),
+                    rhs_scale=xs[:, c, lo:hi],
+                    start=(c == 0),
+                    stop=(c == 1),
+                )
+            if hi == T:
+                if eng == "s":
                     nc.scalar.activation(out=zt[g][:, t, :], in_=zp[f][:], func=ACT.Relu, bias=b_f[:, g, t : t + 1], scale=1.0)
+                else:
+                    nc.vector.tensor_scalar(out=zt[g][:, t, :], in0=zp[f][:], scalar1=b_f[:, g, t : t + 1], scalar2=0.0, op0=ALU.add, op1=ALU.max)
 
         def z_lace(g, h):
-            zi[g, h] = work.tile([P, 256, 4], BF16, name="zi", align_bytes=64)
+            zi[g, h] = work.tile([P, 256, 4], BF16, name="zi", align_bytes=64, bufs=4)
             nc.vector.tensor_copy(out=zi[g, h][:], in_=zt[g][:, :, 256 * h : 256 * (h + 1)].rearrange("p t n -> p n t"))
 
         def z_quant(g, h):
@@ -195,7 +205,7 @@ def tile_sae_encode_decode_fp8_d4_kernel(tc, x_bytes, x_scale, w_enc, b_enc, dec
         def decode(g, b):
             n, h = b // 2, b % 2
             if g == 0:
-                name, bufs = ("rp", EARLY) if b < EARLY else (("tp", TB) if b < EARLY + TB else ("zp", 8 - EARLY - TB))
+                name, bufs = ("rp", EARLY) if b < EARLY else (("tp", TB) if b < EARLY + TB else ("zp", ZB))
                 acc[b] = psum.tile([P, 512], F32, name="acc", tag=name, bufs=bufs)
             nc.tensor.matmul_mx(
                 out=acc[b][:],
@@ -217,48 +227,108 @@ def tile_sae_encode_decode_fp8_d4_kernel(tc, x_bytes, x_scale, w_enc, b_enc, dec
                 )
                 nc.sync.dma_start(out=orows[n][:, 512 * h + w * i : 512 * h + w * (i + 1)], in_=o[:, 0:w])
 
+        warm_up(5)
         x_widen(0)
         nc.scalar.dma_start(out=b_bf[:], in_=b_enc.rearrange("(g p t) -> p g t", p=P, t=4))
         x_widen(1)
         x_turn(0)
+        warm_up(1)
         x_widen(2)
         x_turn(1)
+        warm_up(1)
         x_quant(0)
         x_widen(3)
-        w_turn(0)
+        w_turn(0, True, "s")
+        w_turn(1, True, "v")
         x_quant(1)
         x_turn(2)
+        warm_up(1)
         w_quant(0)
         x_turn(3)
-        w_perm(2)
-        x_quant(2)
-        w_turn(1)
-        nc.scalar.copy(out=b_f[:], in_=b_bf[:])
-        x_quant(3)
-        encode(0, 0, 256)
-        encode(0, 256, 512)
+        warm_up(1)
         w_quant(1)
-        w_perm(3)
-
-        for i in range(2, PAIRS + 3):
-            if i < PAIRS:
-                w_turn(i)
-            if i <= PAIRS:
-                encode(i - 1)
-            if i + 2 < PAIRS and i + 2 >= 4:
-                w_perm(i + 2)
-            if 14 <= i < PAIRS:
-                w_quant(i)
-            if i >= 3:
-                z_lace((i - 3) // 2, (i - 3) % 2)
-            if i < 14:
-                w_quant(i)
-            if i >= 3:
-                z_quant((i - 3) // 2, (i - 3) % 2)
-            if i >= 4 and (i - 4) // 2 < GROUPS - 1:
-                for b in range(EARLY):
-                    if b % 2 == i % 2:
-                        decode((i - 4) // 2, b)
+        w_perm(4)
+        x_quant(2)
+        w_turn(2, True)
+        x_quant(3)
+        nc.scalar.copy(out=b_f[:], in_=b_bf[:])
+        encode(0, 0, 256)
+        encode(1, 0, 256)
+        w_turn(3, True)
+        encode(0, 256, 512)
+        encode(1, 256, 512)
+        w_quant(2)
+        w_perm(5)
+        w_quant(3)
+        w_perm(6)
+        START, FED = 4, 2
+        chunks = [list(range(a, min(a + CHUNK, 32))) for a in range(START, 32, CHUNK)]
+        prev = list(range(FED, START))
+        permed = 7
+        laces, quants, decs = [], [], []
+        for s in range(len(chunks) + 3):
+            now = chunks[s] if s < len(chunks) else []
+            nxt = chunks[s + 1] if s + 1 < len(chunks) else []
+            for f in now:
+                w_turn(f)
+            ready = decs[:]
+            quota = (len(ready) + 1) // 2 if len(ready) <= 2 * EARLY else len(ready)
+            done = []
+            for k in range(0, len(prev), 2):
+                for f in prev[k : k + 2]:
+                    encode(f)
+                for q in range(2):
+                    if ready:
+                        decode(*ready.pop(0))
+                        decs.pop(0)
+            if not prev:
+                while ready:
+                    decode(*ready.pop(0))
+                    decs.pop(0)
+            pre = []
+            for (g, h) in laces:
+                pre.append(("l", g, h))
+            laces = []
+            pm = []
+            while permed < 32 and nxt and permed <= nxt[-1] + PA:
+                pm.append(permed)
+                permed += 1
+            seq = []
+            a, b, c = [("p", f) for f in pm], pre, [("q", f) for f in now]
+            while a or b or c:
+                if a:
+                    seq.append(a.pop(0))
+                if b:
+                    seq.append(b.pop(0))
+                if c and (len(seq) >= 2 or not (a or b)):
+                    seq.append(c.pop(0))
+            zq = quants
+            quants = []
+            for it in seq:
+                if it[0] == "p":
+                    w_perm(it[1])
+                elif it[0] == "l":
+                    z_lace(it[1], it[2])
+                    quants.append((it[1], it[2]))
+                else:
+                    w_quant(it[1])
+                    if zq:
+                        g, h = zq.pop(0)
+                        z_quant(g, h)
+                        if h == 0 and g < GROUPS - 1:
+                            decs += [(g, b) for b in range(EARLY)]
+            for g, h in zq:
+                z_quant(g, h)
+                if h == 0 and g < GROUPS - 1:
+                    decs += [(g, b) for b in range(EARLY)]
+            for f in prev:
+                if f % 4 == 3:
+                    laces += [(f // 4, 0), (f // 4, 1)]
+            prev = now
+        for g, h in quants:
+            z_quant(g, h)
+        for g, b in decs:
+            decode(g, b)
         for b in range(EARLY, EARLY + TB):
             for g in range(GROUPS - 1):
                 decode(g, b)

@@ -100,13 +100,13 @@ def tile_sae_encode_decode_fp8_d4_kernel(tc, x_bytes, x_scale, w_enc, b_enc, dec
 
         xw, xg = {}, {}
 
-        def x_widen(n):
+        def x_widen(n, xv=6):
             xw[n] = work.tile([P, K], BF16, name="xw", bufs=4)
             for b in range(K // B):
                 src = xin[n // 2][:, n % 2, B * b : B * (b + 1)].bitcast(FP8)
                 dst = xw[n][:, B * b : B * (b + 1)]
                 s = xsc[:, n, b : b + 1]
-                if b < XV:
+                if b < xv:
                     nc.vector.tensor_scalar(out=dst, in0=src, scalar1=s, scalar2=None, op0=ALU.mult)
                 else:
                     nc.scalar.activation(out=dst, in_=src, func=ACT.Copy, scale=s)
@@ -190,7 +190,10 @@ def tile_sae_encode_decode_fp8_d4_kernel(tc, x_bytes, x_scale, w_enc, b_enc, dec
 
         def z_lace(g, h):
             zi[g, h] = work.tile([P, 256, 4], BF16, name="zi", align_bytes=64, bufs=4)
-            nc.vector.tensor_copy(out=zi[g, h][:], in_=zt[g][:, :, 256 * h : 256 * (h + 1)].rearrange("p t n -> p n t"))
+            nc.vector.tensor_copy(
+                out=zi[g, h][:].rearrange("p (c i) t -> p c t i", i=4),
+                in_=zt[g][:, :, 256 * h : 256 * (h + 1)].rearrange("p t (c i) -> p c t i", i=4),
+            )
 
         def z_quant(g, h):
             nc.vector.quantize_mx(
@@ -228,36 +231,33 @@ def tile_sae_encode_decode_fp8_d4_kernel(tc, x_bytes, x_scale, w_enc, b_enc, dec
                 nc.sync.dma_start(out=orows[n][:, 512 * h + w * i : 512 * h + w * (i + 1)], in_=o[:, 0:w])
 
         warm_up(5)
-        x_widen(0)
+        x_widen(0, 5)
         nc.scalar.dma_start(out=b_bf[:], in_=b_enc.rearrange("(g p t) -> p g t", p=P, t=4))
-        x_widen(1)
-        x_turn(0)
+        x_turn(0, "s")
+        x_widen(1, 8)
+        x_widen(2, 7)
+        w_turn(0, True, "s")
+        x_widen(3, 8)
+        x_turn(1, "v")
+        w_turn(1, True, "s")
         warm_up(1)
-        x_widen(2)
-        x_turn(1)
+        x_turn(2, "s")
+        x_turn(3, "s")
         warm_up(1)
         x_quant(0)
-        x_widen(3)
-        w_turn(0, True, "s")
-        w_turn(1, True, "v")
         x_quant(1)
-        x_turn(2)
-        warm_up(1)
         w_quant(0)
-        x_turn(3)
-        warm_up(1)
-        w_quant(1)
-        w_perm(4)
-        x_quant(2)
-        w_turn(2, True)
-        x_quant(3)
+        w_turn(2, True, "s")
         nc.scalar.copy(out=b_f[:], in_=b_bf[:])
-        encode(0, 0, 256)
-        encode(1, 0, 256)
-        w_turn(3, True)
-        encode(0, 256, 512)
-        encode(1, 256, 512)
+        w_quant(1)
+        x_quant(2)
+        x_quant(3)
         w_quant(2)
+        w_turn(3, True, "s")
+        warm_up(1)
+        encode(0)
+        w_perm(4)
+        encode(1)
         w_perm(5)
         w_quant(3)
         w_perm(6)

from contextlib import ExitStack

import concourse.mybir as mybir
from concourse.masks import make_identity

T, K, F, B = 512, 1024, 4096, 128
FLOPS = 2 * 2 * T * K * F

F32 = mybir.dt.float32
BF16 = mybir.dt.bfloat16
I32 = mybir.dt.int32
U32 = mybir.dt.uint32
U8 = mybir.dt.uint8
FP8 = mybir.dt.float8_e4m3fn
FP8X4 = mybir.dt.float8_e4m3fn_x4
FP4X4 = mybir.dt.float4_e2m1fn_x4
ALU = mybir.AluOpType
ACT = mybir.ActivationFunctionType

P = 128
GROUPS = F // 512
PAIRS = F // 256
CHUNK = 2
ZB = 2
PA = 1
EARLY = 8 - CHUNK - ZB
TB = CHUNK
XV = 6
DIRECT = 2


def tile_sae_encode_decode_fp8_d4_kernel(tc, x_bytes, x_scale, w_enc, b_enc, dec_words, dec_scales, b_dec, out):
    nc = tc.nc
    with ExitStack() as ctx:
        keep = ctx.enter_context(tc.tile_pool(name="keep", bufs=1))
        wraw = ctx.enter_context(tc.tile_pool(name="wraw", bufs=PAIRS))
        work = ctx.enter_context(tc.tile_pool(name="work", bufs=3))
        outp = ctx.enter_context(tc.tile_pool(name="outp", bufs=4))
        psum = ctx.enter_context(tc.psum_pool(name="psum", bufs=2))

        ident = keep.tile([P, P], F32, name="ident")
        dsc = keep.tile([P, GROUPS, K], U8, name="dsc", align_bytes=64)
        dw = keep.tile([P, GROUPS, 2 * K], U8, name="dw", align_bytes=64)
        zc = keep.tile([P, GROUPS, T], U32, name="zc", align_bytes=64)
        zs = keep.tile([P, GROUPS, T], U8, name="zs", align_bytes=64)
        xc = keep.tile([P, 2, T], U32, name="xc", align_bytes=64)
        xs = keep.tile([P, 2, T], U8, name="xs", align_bytes=64)
        xsc = keep.tile([P, 4, 8], F32, name="xsc")
        b_bf = keep.tile([P, GROUPS, 4], BF16, name="b_bf")
        b_f = keep.tile([P, GROUPS, 4], F32, name="b_f")
        bd = keep.tile([P, K], BF16, name="bd")
        xin = [keep.tile([P, 2, K], U8, name="xin%d" % i) for i in range(2)]

        ctx.enter_context(tc.manual_schedule())

        make_identity(nc, ident[:])
        warm = keep.tile([P, 512], BF16, name="warm")
        nc.vector.memset(warm[:], 0.0)

        def warm_up(n):
            for i in range(n):
                wp = psum.tile([P, T], F32, name="wp", tag="zp", bufs=ZB)
                nc.tensor.matmul(wp[:], lhsT=warm[:, 0:P], rhs=warm[:], start=True, stop=True)

        nc.vector.memset(dsc[:].rearrange("p g n -> p (g n)").bitcast(I32), 0)

        nc.sync.dma_start(out=xsc[:], in_=x_scale.rearrange("(p n) b -> p n b", p=P))

        xr = x_bytes.rearrange("(p i n) k -> i p n k", p=P, n=2)
        wr = w_enc.rearrange("(g m t) k -> g m t k", m=P, t=4)
        raws = []

        def load_w(j):
            raw = wraw.tile([P, 2, K], BF16, name="raw")
            t0 = 2 * (j % 2)
            nc.sync.dma_start(out=raw[:], in_=wr[j // 2][:, t0 : t0 + 2, :])
            raws.append(raw)

        def load_dec(g):
            nc.sync.dma_start(out=dw[:, g, :].bitcast(I32), in_=dec_words[g].bitcast(I32))

        for i in range(2):
            nc.sync.dma_start(out=xin[i][:], in_=xr[i])
            if i == 0:
                load_w(0)
        for j in range(1, 6):
            load_w(j)
        for q in range(4):
            nc.sync.dma_start(
                out=dsc[32 * q : 32 * q + 4, :, :].bitcast(I32),
                in_=dec_scales[:, 4 * q : 4 * q + 4, :].rearrange("g q n -> q g n").bitcast(I32),
            )
        load_dec(0)
        for j in range(6, PAIRS):
            load_w(j)
            if j - 5 < GROUPS:
                load_dec(j - 5)
        nc.sync.dma_start(out=bd[:], in_=b_dec.partition_broadcast(P))


        xw, xg = {}, {}

        def x_widen(n, xv=6):
            xw[n] = work.tile([P, K], BF16, name="xw", bufs=4)
            for b in range(K // B):
                src = xin[n // 2][:, n % 2, B * b : B * (b + 1)].bitcast(FP8)
                dst = xw[n][:, B * b : B * (b + 1)]
                s = xsc[:, n, b : b + 1]
                if b < xv:
                    nc.vector.tensor_scalar(out=dst, in0=src, scalar1=s, scalar2=None, op0=ALU.mult)
                else:
                    nc.scalar.activation(out=dst, in_=src, func=ACT.Copy, scale=s)

        def words_out(dst, bank, eng="s"):
            if eng == "s":
                nc.scalar.copy(out=dst, in_=bank)
            else:
                nc.vector.tensor_copy(out=dst, in_=bank)

        def x_turn(n, eng="s"):
            tp = psum.tile([P, 2, 2, P], F32, name="xp", tag="rp", bufs=EARLY)
            words = xw[n][:].bitcast(F32)
            for c in range(2):
                for u in range(2):
                    nc.tensor.transpose(tp[:, c, u, :], words[:, 256 * c + u : 256 * (c + 1) : 2], ident[:])
            xg[n] = work.tile([P, 2, P, 4], BF16, name="xg", bufs=4, align_bytes=64)
            dst = xg[n][:].rearrange("p c r t -> p (c r t)").bitcast(F32).rearrange("p (c r u) -> p c r u", c=2, u=2)
            words_out(dst, tp[:].rearrange("p c u r -> p c r u"), eng)

        def x_quant(n):
            for c in range(2):
                nc.vector.quantize_mx(
                    out=xc[:, c, P * n : P * (n + 1)].bitcast(FP8X4),
                    scales=xs[:, c, P * n : P * (n + 1)],
                    in_=xg[n][:, c, :, :].rearrange("p r t -> p (r t)"),
                )

        perm, wg, wc, ws = {}, {}, {}, {}

        def raw_words(f):
            return raws[f // 2][:, f % 2, :].bitcast(F32)

        def w_perm(f):
            perm[f] = work.tile([P, 2, 2, P], F32, name="perm", bufs=6)
            nc.vector.tensor_copy(out=perm[f][:], in_=raw_words(f).rearrange("p (c m u) -> p c u m", m=P, u=2))

        def w_turn(f, direct=False, eng="s", tag="tp", bufs=TB):
            wg[f] = work.tile([P, 2, P, 4], BF16, name="wg", align_bytes=64, bufs=8)
            tp = psum.tile([P, 2, 2, P], F32, name="tp", tag=tag, bufs=bufs)
            for c in range(2):
                for u in range(2):
                    src = raw_words(f)[:, 256 * c + u : 256 * (c + 1) : 2] if direct else perm[f][:, c, u, :]
                    nc.tensor.transpose(tp[:, c, u, :], src, ident[:])
            dst = wg[f][:].rearrange("p c r t -> p (c r t)").bitcast(F32).rearrange("p (c r u) -> p c r u", c=2, u=2)
            words_out(dst, tp[:].rearrange("p c u r -> p c r u"), eng)

        def w_quant(f):
            wc[f] = work.tile([P, 2, P], U32, name="wc", align_bytes=64, bufs=8)
            ws[f] = work.tile([P, 2, P], U8, name="ws", align_bytes=64, bufs=8)
            nc.vector.quantize_mx(
                out=wc[f][:].rearrange("p x r -> p (x r)").bitcast(FP8X4),
                scales=ws[f][:].rearrange("p x r -> p (x r)"),
                in_=wg[f][:].rearrange("p c r t -> p (c r t)"),
            )

        zt, zi = {}, {}
        zp = {}

        def encode(f, lo=0, hi=T, eng="s"):
            g, t = f // 4, f % 4
            if t == 0 and lo == 0:
                zt[g] = work.tile([P, 4, T], BF16, name="zt")
            if lo == 0:
                zp[f] = psum.tile([P, T], F32, name="zp", bufs=ZB)
            for c in range(2):
                nc.tensor.matmul_mx(
                    out=zp[f][:, lo:hi],
                    lhsT=wc[f][:, c, :].bitcast(FP8X4),
                    lhsT_scale=ws[f][:, c, :],
                    rhs=xc[:, c, lo:hi].bitcast(FP8X4),
                    rhs_scale=xs[:, c, lo:hi],
                    start=(c == 0),
                    stop=(c == 1),
                )
            if hi == T:
                if eng == "s":
                    nc.scalar.activation(out=zt[g][:, t, :], in_=zp[f][:], func=ACT.Relu, bias=b_f[:, g, t : t + 1], scale=1.0)
                else:
                    nc.vector.tensor_scalar(out=zt[g][:, t, :], in0=zp[f][:], scalar1=b_f[:, g, t : t + 1], scalar2=0.0, op0=ALU.add, op1=ALU.max)

        def z_lace(g, h):
            zi[g, h] = work.tile([P, 256, 4], BF16, name="zi", align_bytes=64, bufs=4)
            nc.vector.tensor_copy(
                out=zi[g, h][:].rearrange("p (c i) t -> p c t i", i=4),
                in_=zt[g][:, :, 256 * h : 256 * (h + 1)].rearrange("p t (c i) -> p c t i", i=4),
            )

        def z_quant(g, h):
            nc.vector.quantize_mx(
                out=zc[:, g, 256 * h : 256 * (h + 1)].bitcast(FP8X4),
                scales=zs[:, g, 256 * h : 256 * (h + 1)],
                in_=zi[g, h][:].rearrange("p n t -> p (n t)"),
            )

        acc = {}
        orows = out.rearrange("(p n) k -> n p k", p=P)

        def decode(g, b):
            n, h = b // 2, b % 2
            if g == 0:
                name, bufs = ("rp", EARLY) if b < EARLY else (("tp", TB) if b < EARLY + TB else ("zp", ZB))
                acc[b] = psum.tile([P, 512], F32, name="acc", tag=name, bufs=bufs)
            nc.tensor.matmul_mx(
                out=acc[b][:],
                lhsT=zc[:, g, P * n : P * (n + 1)].bitcast(FP8X4),
                lhsT_scale=zs[:, g, P * n : P * (n + 1)],
                rhs=dw[:, g, 1024 * h : 1024 * (h + 1)].bitcast(FP4X4),
                rhs_scale=dsc[:, g, 512 * h : 512 * (h + 1)],
                start=(g == 0),
                stop=(g == GROUPS - 1),
            )

        def store(b, cuts):
            n, h = b // 2, b % 2
            w = 512 // cuts
            for i in range(cuts):
                o = outp.tile([P, 512], F32, name="o")
                nc.vector.tensor_tensor(
                    out=o[:, 0:w], in0=acc[b][:, w * i : w * (i + 1)], in1=bd[:, 512 * h + w * i : 512 * h + w * (i + 1)], op=ALU.add
                )
                nc.sync.dma_start(out=orows[n][:, 512 * h + w * i : 512 * h + w * (i + 1)], in_=o[:, 0:w])

        warm_up(5)
        x_widen(0, 5)
        nc.scalar.dma_start(out=b_bf[:], in_=b_enc.rearrange("(g p t) -> p g t", p=P, t=4))
        x_turn(0, "s")
        x_widen(1, 8)
        x_widen(2, 7)
        w_turn(0, True, "s")
        x_widen(3, 8)
        x_turn(1, "v")
        w_turn(1, True, "s")
        warm_up(1)
        x_turn(2, "s")
        x_turn(3, "s")
        warm_up(1)
        x_quant(0)
        x_quant(1)
        w_quant(0)
        w_turn(2, True, "s")
        nc.scalar.copy(out=b_f[:], in_=b_bf[:])
        w_quant(1)
        x_quant(2)
        x_quant(3)
        w_quant(2)
        w_turn(3, True, "s")
        warm_up(1)
        encode(0)
        w_perm(4)
        encode(1)
        w_perm(5)
        w_quant(3)
        w_perm(6)
        START, FED = 4, 2
        chunks = [list(range(a, min(a + CHUNK, 32))) for a in range(START, 32, CHUNK)]
        prev = list(range(FED, START))
        permed = 7
        laces, quants, decs = [], [], []
        for s in range(len(chunks) + 3):
            now = chunks[s] if s < len(chunks) else []
            nxt = chunks[s + 1] if s + 1 < len(chunks) else []
            for f in now:
                w_turn(f)
            ready = decs[:]
            quota = (len(ready) + 1) // 2 if len(ready) <= 2 * EARLY else len(ready)
            done = []
            for k in range(0, len(prev), 2):
                for f in prev[k : k + 2]:
                    encode(f)
                for q in range(2):
                    if ready:
                        decode(*ready.pop(0))
                        decs.pop(0)
            if not prev:
                while ready:
                    decode(*ready.pop(0))
                    decs.pop(0)
            pre = []
            for (g, h) in laces:
                pre.append(("l", g, h))
            laces = []
            pm = []
            while permed < 32 and nxt and permed <= nxt[-1] + PA:
                pm.append(permed)
                permed += 1
            seq = []
            a, b, c = [("p", f) for f in pm], pre, [("q", f) for f in now]
            while a or b or c:
                if a:
                    seq.append(a.pop(0))
                if b:
                    seq.append(b.pop(0))
                if c and (len(seq) >= 2 or not (a or b)):
                    seq.append(c.pop(0))
            zq = quants
            quants = []
            for it in seq:
                if it[0] == "p":
                    w_perm(it[1])
                elif it[0] == "l":
                    z_lace(it[1], it[2])
                    quants.append((it[1], it[2]))
                else:
                    w_quant(it[1])
                    if zq:
                        g, h = zq.pop(0)
                        z_quant(g, h)
                        if h == 0 and g < GROUPS - 1:
                            decs += [(g, b) for b in range(EARLY)]
            for g, h in zq:
                z_quant(g, h)
                if h == 0 and g < GROUPS - 1:
                    decs += [(g, b) for b in range(EARLY)]
            for f in prev:
                if f % 4 == 3:
                    laces += [(f // 4, 0), (f // 4, 1)]
            prev = now
        for g, h in quants:
            z_quant(g, h)
        for g, b in decs:
            decode(g, b)
        for b in range(EARLY, EARLY + TB):
            for g in range(GROUPS - 1):
                decode(g, b)
        for b in range(EARLY + TB):
            decode(GROUPS - 1, b)
            store(b, 1)
        for b in range(EARLY + TB, 8):
            for g in range(GROUPS):
                decode(g, b)
            store(b, 2 if b == 7 else 1)
